import numpy as np, ml_dtypes
CORES = [36,38,116,118,124,126,164,166,244,246,252,254]
N = 12
import mx_ref
NC, G = 128, 4
C = np.float32(0.037)
BF = ml_dtypes.bfloat16
def cut(t, i, w=512):
    return t[:, w * i:w * i + w]
def tile(rs):
    return np.stack(rs, axis=2).reshape(128, -1).astype(BF)
def layer(w, X):
    out = []
    for i in range(G):
        for t in range(len(X)):
            p = mx_ref.matmul(mx_ref.quantize(cut(w, len(X) * i + t)), X[t])
            z = p if t == 0 else z + p
        out.append(z)
    return out
def act(Z):
    return [np.maximum(z, 0) * C for z in Z]
def setup_inputs(rng):
    def f(*shape):
        return mx_ref.flush((rng.standard_normal(shape, dtype=np.float32) * np.exp2(rng.integers(-2, 3, shape[:-1] + (1,)))).astype(BF))
    return {"xk": f(N, 128, 512), "xq": f(N, 128, 4 * NC), "wk": f(N, 128, G * 512), "wq": f(N, 128, G * 512)}
def setup_inputs_blocks(rng):
    d = setup_inputs(rng)
    for k in ("xk", "xq", "wk", "wq"): d[k] = mx_ref.spread(d[k], rng, 4)
    return d
def setup_inputs_wide(rng):
    d = setup_inputs(rng)
    for k in ("xk", "xq", "wk", "wq"): d[k] = mx_ref.flush((d[k].astype(np.float32) * np.exp2(rng.integers(-5, 6, (N, 1, 1))).astype(np.float32)).astype(BF))
    return d
def reference(xk, xq, wk, wq):
    K = [mx_ref.quantize(tile(act(layer(wk[j], [mx_ref.quantize(xk[j])])))) for j in range(N)]
    y = np.zeros((N, 128, N * NC), np.float32)
    for r in range(N):
        q = mx_ref.quantize(tile(act(layer(wq[r], [mx_ref.quantize(xq[r])]))))
        for j in range(N):
            y[r][:, NC * j:NC * j + NC] = mx_ref.matmul(K[j], q)
    return {"y": y}

@@ -1,0 +1,297 @@
+from concourse.bass import DstId, RemoteDMATransfer
+from concourse.mybir import dt, AluOpType, ActivationFunctionType
+
+N, NC, G = 12, 128, 4
+TILE = 4 * NC
+WORLD = 256
+CONST = 0.037
+BANK, NBANK = 512, 8
+PER_RELAY = 2
+BATCHES = 1
+MOVE = 1
+
+SCRATCH = {
+    "xkb": ("sbuf", [128, TILE], "bfloat16"), "wkb": ("sbuf", [128, G * TILE], "bfloat16"),
+    "xqb": ("sbuf", [128, TILE], "bfloat16"), "wqb": ("sbuf", [128, G * TILE], "bfloat16"),
+    "xkc": ("sbuf", [128, NC], "float8_e4m3fn_x4"), "xks": ("sbuf", [128, NC], "uint8"),
+    "wkc": ("sbuf", [128, G * NC], "float8_e4m3fn_x4"), "wks": ("sbuf", [128, G * NC], "uint8"),
+    "xqc": ("sbuf", [128, NC], "float8_e4m3fn_x4"), "xqs": ("sbuf", [128, NC], "uint8"),
+    "wqc": ("sbuf", [128, G * NC], "float8_e4m3fn_x4"), "wqs": ("sbuf", [128, G * NC], "uint8"),
+    "kt": ("sbuf", [128, TILE], "bfloat16"), "qt": ("sbuf", [128, TILE], "bfloat16"),
+    "kc": ("sbuf", [128, N * NC], "float8_e4m3fn_x4"), "ks": ("sbuf", [128, N * NC], "uint8"),
+    "qc": ("sbuf", [128, NC], "float8_e4m3fn_x4"), "qs": ("sbuf", [128, NC], "uint8"),
+    "ysb": ("sbuf", [128, N * NC], "float32"),
+    "ps": ("psum", [128, NBANK * BANK], "float32"),
+}
+SEMAPHORES = (
+    ["lxk", "lwk0", "lwk1", "lxq", "lwq0", "lwq1", "vxk", "vxq", "vk", "vq", "ak", "aq", "ls", "st"]
+    + ["vwk%d" % i for i in range(G)] + ["vwq%d" % i for i in range(G)]
+    + ["mk%d" % i for i in range(G)] + ["mq%d" % i for i in range(G)]
+    + ["my%d" % j for j in range(N)] + ["cy%d" % j for j in range(N)]
+    + ["a%d" % j for j in range(N)] + ["s%d" % j for j in range(N)] + ["fw%d" % b for b in range(4)]
+)
+KINDS = ((True, "s%d"), (False, "a%d"))
+_MEMO = {}
+
+
+def _bits(m):
+    return [b for b in range(m.bit_length()) if (m >> b) & 1]
+
+
+def _pow2(n):
+    p = 1
+    while p * 2 <= n:
+        p *= 2
+    return p
+
+
+def _mask(bits):
+    return sum(1 << b for b in bits)
+
+
+def _common(topo, src, dsts):
+    m = topo.mask(src, dsts[0])
+    for d in dsts[1:]:
+        m &= topo.mask(src, d)
+    return _bits(m)
+
+
+def _split(seq, parts):
+    parts = max(1, min(parts, len(seq)))
+    out, at = [], 0
+    for p in range(parts):
+        n = (len(seq) - at + (parts - p) - 1) // (parts - p)
+        out.append(seq[at:at + n])
+        at += n
+    return out
+
+
+def _plan(topo, cores):
+    def place(c):
+        return (topo.host(c), topo.chip(c))
+    chips = []
+    for c in cores:
+        if place(c) not in chips:
+            chips.append(place(c))
+    on = {k: [c for c in cores if place(c) == k] for k in chips}
+    idle = {k: [c for c in range(WORLD) if place(c) == k and c not in cores] for k in chips}
+    other = {c: [d for d in on[place(c)] if d != c][0] for c in cores}
+    tile = {c: j for j, c in enumerate(cores)}
+    once = {k: [] for k in chips}
+    twice = {k: [] for k in chips}
+    reach, shut = {}, {}
+    for s in cores:
+        i = chips.index(place(s))
+        ring = [chips[(i + 1 + t) % len(chips)] for t in range(len(chips) - 1)]
+        reach[s] = [k for k in ring if all(topo.may_write(s, d) for d in on[k])]
+        shut[s] = [k for k in ring if k not in reach[s]]
+        for k in shut[s]:
+            twice[k].append(tile[s])
+    lent = {s: [] for s in cores}
+    for s in cores:
+        p = other[s]
+        for _ in range(MOVE):
+            can = [k for k in reach[s] if k in reach[p]]
+            if can and len(reach[s]) - len(reach[p]) - len(lent[p]) >= 2:
+                reach[s].remove(can[-1])
+                lent[p].append(can[-1])
+    for s in cores:
+        for turn, k in enumerate(reach[s]):
+            once[k].append((tile[s], turn))
+        for turn, k in enumerate(lent[s]):
+            once[k].append((tile[other[s]], len(reach[s]) + turn))
+    land, ranks = {}, {}
+    for k in chips:
+        lst = sorted(once[k])
+        half = (len(lst) + 1) // 2
+        for n, (j, turn) in enumerate(lst):
+            land[(k, j)] = on[k][0] if n < half else on[k][1]
+    for k in chips:
+        turn_of = dict(once[k])
+        for c in on[k]:
+            mine = sorted([j for j, _ in once[k] if land[(k, j)] == c], key=lambda j: (turn_of[j], j))
+            ranks[c] = {"tile": tile[c], "partner": other[c], "mine": mine, "twice": sorted(twice[k]), "need": {}}
+    for c in cores:
+        e, p = ranks[c], ranks[other[c]]
+        order = [e["tile"]] + e["mine"] + [p["tile"]] + p["mine"] + e["twice"]
+        e["slot"] = {j: n for n, j in enumerate(order)}
+        e["theirs"] = list(p["mine"])
+    relays = {}
+    for s in cores:
+        e, j, pj, k = ranks[s], tile[s], tile[other[s]], place(s)
+        helpers = []
+        if shut[s]:
+            far = [d for kk in shut[s] for d in on[kk]]
+            can = [h for h in idle[k] if h not in relays and all(topo.may_write(h, d) for d in far)]
+            can.sort(key=lambda h: (topo.die(h) == topo.die(s), h))
+            for part in _split(far, min(len(can), (len(far) + PER_RELAY - 1) // PER_RELAY)):
+                h = can.pop(0)
+                bits = _common(topo, h, part)
+                bits = bits[:_pow2(len(bits))]
+                relays[h] = {"tile": j, "dsts": [(d, ranks[d]["slot"][j]) for d in part], "bits": bits}
+                for d in part:
+                    ranks[d]["need"][j] = len(bits)
+                helpers.append(h)
+        e["off"] = [(land[(kk, j)], ranks[land[(kk, j)]]["slot"][j]) for kk in reach[s]]
+        e["lent"] = [(land[(kk, pj)], ranks[land[(kk, pj)]]["slot"][pj]) for kk in lent[s]]
+        e["near"] = [(h, 0) for h in helpers] + [(other[s], ranks[other[s]]["slot"][j])]
+        off = _common(topo, s, [d for d, _ in e["off"] + e["lent"]])
+        off = off[:_pow2(len(off))]
+        near = [b for b in _common(topo, s, [d for d, _ in e["near"]]) if b not in off]
+        near = near[:_pow2(len(near))]
+        e["off_bits"], e["near_bits"] = off, near
+        for d, _ in e["off"]:
+            ranks[d]["need"][j] = len(off)
+        for d, _ in e["lent"]:
+            ranks[d]["need"][pj] = len(off)
+        ranks[other[s]]["need"][j] = len(near)
+        for h in helpers:
+            relays[h]["need"] = len(near)
+        fw = _common(topo, s, [other[s]])
+        e["fw_bits"] = fw[:_pow2(len(fw))]
+        e["fw_slot"] = {t: ranks[other[s]]["slot"][t] for t in e["mine"]}
+    return {"ranks": ranks, "relays": relays}
+
+
+def _view(T, plane, slot, width):
+    a, b = NC * slot, NC * (slot + width)
+    return T.ks[:, a:b] if plane else T.kc[:, a:b].bitcast(dt.uint8)
+
+
+def _send(g, T, topo, core, plane, groups, width, sent):
+    trs = []
+    for bits, s0, dsts, sem in groups:
+        ids = []
+        for d, _ in dsts:
+            rid, pid = topo.addr(d, core)
+            ids.append(DstId(rid=rid, pnc=pid))
+        trs.append(RemoteDMATransfer(dst_ids=ids, dma_engine_mask=_mask(bits), remote_sem=T.sem[sem],
+                                     srcs=[_view(T, plane, s0, width)],
+                                     dsts=[_view(T, plane, d0, width) for _, d0 in dsts]))
+        sent[0] += len(bits)
+    g.remote_dma_fused(trs, local_sem=T.sem.ls)
+
+
+def _relay(g, core, T, topo, r):
+    sent = [0]
+    for plane, sem in KINDS:
+        g.wait_ge(T.sem[sem % r["tile"]], r["need"])
+        _send(g, T, topo, core, plane, [(r["bits"], 0, r["dsts"], sem % r["tile"])], 1, sent)
+    g.wait_ge(T.sem.ls, sent[0])
+
+
+def _layer(g, T, x):
+    S, V, A, P = T.sem, g.vector, g.scalar, g.tensor
+    xb, wb, xc, xs, wc, ws, tl = (T["x%sb" % x], T["w%sb" % x], T["x%sc" % x], T["x%ss" % x], T["w%sc" % x], T["w%ss" % x],
+                                  T["%st" % x])
+    base = 0 if x == "k" else G
+    V.wait_ge(S["lx%s" % x], 16)
+    V.quantize_mx(xc[:], xs[:], xb[:]).then_inc(S["vx%s" % x], 1)
+    P.wait_ge(S["vx%s" % x], 1)
+    for i in range(G):
+        if i % 2 == 0:
+            V.wait_ge(S["lw%s%d" % (x, i // 2)], 16)
+        V.quantize_mx(wc[:, NC * i:NC * i + NC], ws[:, NC * i:NC * i + NC],
+                      wb[:, TILE * i:TILE * i + TILE]).then_inc(S["vw%s%d" % (x, i)], 1)
+        P.wait_ge(S["vw%s%d" % (x, i)], 1)
+        P.matmul_mx(T.ps[:, BANK * (base + i):BANK * (base + i) + NC], wc[:, NC * i:NC * i + NC], ws[:, NC * i:NC * i + NC],
+                    xc[:], xs[:], True, True).then_inc(S["m%s%d" % (x, i)], 1)
+    for i in range(G):
+        z = T.ps[:, BANK * (base + i):BANK * (base + i) + NC]
+        if i % 2 == 0:
+            A.wait_ge(S["m%s%d" % (x, i)], 1)
+            A.activation(tl[:, i:TILE:4], z, ActivationFunctionType.Relu, scale=CONST).then_inc(S["a%s" % x], 1)
+        else:
+            V.wait_ge(S["m%s%d" % (x, i)], 1)
+            V.tensor_scalar(tl[:, i:TILE:4], z, 0.0, CONST, AluOpType.max, AluOpType.mult).then_inc(S["a%s" % x], 1)
+    V.wait_ge(S["a%s" % x], G)
+    if x == "k":
+        V.quantize_mx(T.kc[:, 0:NC], T.ks[:, 0:NC], tl[:]).then_inc(S.vk, 1)
+    else:
+        V.quantize_mx(T.qc[:], T.qs[:], tl[:]).then_inc(S.vq, 1)
+
+
+def _runs(tiles):
+    out = []
+    for j in sorted(tiles):
+        if out and out[-1][-1] == j - 1:
+            out[-1].append(j)
+        else:
+            out.append([j])
+    return out
+
+
+def _rank(g, core, T, topo, e, pt):
+    S, V, A, P, D = T.sem, g.vector, g.scalar, g.tensor, g.sync
+    H = G * TILE // 2
+    me = e["tile"]
+    D.dma_start(T.xkb[:], T.xk[:]).then_inc(S.lxk, 16)
+    A.dma_start(T.wkb[:, 0:H], T.wk[:, 0:H]).then_inc(S.lwk0, 16)
+    D.dma_start(T.wkb[:, H:2 * H], T.wk[:, H:2 * H]).then_inc(S.lwk1, 16)
+    D.wait_ge(S.lxk, 16)
+    D.wait_ge(S.lwk1, 16)
+    D.dma_start(T.xqb[:], T.xq[:]).then_inc(S.lxq, 16)
+    D.dma_start(T.wqb[:, 0:H], T.wq[:, 0:H]).then_inc(S.lwq0, 16)
+    D.dma_start(T.wqb[:, H:2 * H], T.wq[:, H:2 * H]).then_inc(S.lwq1, 16)
+    _layer(g, T, "k")
+    sent = [0]
+    g.wait_ge(S.vk, 1)
+    for plane, sem in KINDS:
+        _send(g, T, topo, core, plane, [(e["off_bits"], 0, e["off"], sem % me), (e["near_bits"], 0, e["near"], sem % me)], 1, sent)
+    _layer(g, T, "q")
+    if e["lent"]:
+        for plane, sem in KINDS:
+            g.wait_ge(S[sem % pt], e["need"][pt])
+            _send(g, T, topo, core, plane, [(e["off_bits"], e["slot"][pt], e["lent"], sem % pt)], 1, sent)
+    for plane, sem in KINDS:
+        for b, part in enumerate(_split(e["mine"], BATCHES)):
+            for j in part:
+                g.wait_ge(S[sem % j], e["need"][j])
+            _send(g, T, topo, core, plane,
+                  [(e["fw_bits"], e["slot"][part[0]], [(e["partner"], e["fw_slot"][part[0]])], "fw%d" % b)], len(part), sent)
+    g.wait_ge(S.ls, sent[0])
+    came = {me: ("vk", 1)}
+    for j in [pt] + e["mine"] + e["twice"]:
+        came[j] = ("a%d" % j, e["need"][j])
+    for b, part in enumerate(_split(e["theirs"], BATCHES)):
+        for j in part:
+            came[j] = ("fw%d" % b, 2 * len(e["fw_bits"]))
+    order = [me, pt] + e["mine"] + e["twice"] + e["theirs"]
+    P.wait_ge(S.vq, 1)
+    P.wait_ge(S.ak, G)
+    P.wait_ge(S.aq, G)
+    for n, j in enumerate(order):
+        P.wait_ge(S[came[j][0]], came[j][1])
+        if came[j][0] == "a%d" % j:
+            P.wait_ge(S["s%d" % j], came[j][1])
+        if n >= NBANK:
+            P.wait_ge(S["cy%d" % order[n - NBANK]], 1)
+        z = T.ps[:, BANK * (n % NBANK):BANK * (n % NBANK) + NC]
+        s = e["slot"][j]
+        P.matmul_mx(z, T.kc[:, NC * s:NC * s + NC], T.ks[:, NC * s:NC * s + NC], T.qc[:], T.qs[:], True, True
+                    ).then_inc(S["my%d" % j], 1)
+        out = T.ysb[:, NC * j:NC * j + NC]
+        if n % 2 == 0:
+            V.wait_ge(S["my%d" % j], 1)
+            V.tensor_copy(out, z).then_inc(S["cy%d" % j], 1)
+        else:
+            A.wait_ge(S["my%d" % j], 1)
+            A.activation(out, z, ActivationFunctionType.Copy).then_inc(S["cy%d" % j], 1)
+    runs = _runs([me, pt]) + _runs(e["mine"]) + _runs(e["twice"] + e["theirs"])
+    runs.sort(key=lambda r: max(order.index(j) for j in r))
+    for r in runs:
+        for j in r:
+            D.wait_ge(S["cy%d" % j], 1)
+        D.dma_start(T.y[:, NC * r[0]:NC * r[-1] + NC], T.ysb[:, NC * r[0]:NC * r[-1] + NC]).then_inc(S.st, 16)
+    D.wait_ge(S.st, 16 * len(runs))
+
+
+def rank_program(g, core, T, topo):
+    if "plan" not in _MEMO:
+        _MEMO["plan"] = _plan(topo, list(T.cores))
+    plan = _MEMO["plan"]
+    if core in plan["relays"]:
+        _relay(g, core, T, topo, plan["relays"][core])
+    elif core in plan["ranks"]:
+        e = plan["ranks"][core]
+        _rank(g, core, T, topo, e, plan["ranks"][e["partner"]]["tile"])

@@ -6,9 +6,8 @@ TILE = 4 * NC
 WORLD = 256
 CONST = 0.037
 BANK, NBANK = 512, 8
-PER_RELAY = 2
-BATCHES = 1
-MOVE = 1
+SELF = 3
+HOP, FWD = 3.0, 1.5
 
 SCRATCH = {
     "xkb": ("sbuf", [128, TILE], "bfloat16"), "wkb": ("sbuf", [128, G * TILE], "bfloat16"),
@@ -24,11 +23,11 @@ SCRATCH = {
     "ps": ("psum", [128, NBANK * BANK], "float32"),
 }
 SEMAPHORES = (
-    ["lxk", "lwk0", "lwk1", "lxq", "lwq0", "lwq1", "vxk", "vxq", "vk", "vq", "ak", "aq", "ls", "st"]
+    ["lxk", "lwk0", "lwk1", "lxq", "lwq0", "lwq1", "vxk", "vxq", "vk", "vq", "ak", "aq", "ls", "st", "fp0", "fp1"]
     + ["vwk%d" % i for i in range(G)] + ["vwq%d" % i for i in range(G)]
     + ["mk%d" % i for i in range(G)] + ["mq%d" % i for i in range(G)]
     + ["my%d" % j for j in range(N)] + ["cy%d" % j for j in range(N)]
-    + ["a%d" % j for j in range(N)] + ["s%d" % j for j in range(N)] + ["fw%d" % b for b in range(4)]
+    + ["a%d" % j for j in range(N)] + ["s%d" % j for j in range(N)] + ["fw%d" % b for b in range(N)]
 )
 KINDS = ((True, "s%d"), (False, "a%d"))
 _MEMO = {}
@@ -53,7 +52,8 @@ def _common(topo, src, dsts):
     m = topo.mask(src, dsts[0])
     for d in dsts[1:]:
         m &= topo.mask(src, d)
-    return _bits(m)
+    b = _bits(m)
+    return b[:_pow2(len(b))]
 
 
 def _split(seq, parts):
@@ -74,81 +74,82 @@ def _plan(topo, cores):
         if place(c) not in chips:
             chips.append(place(c))
     on = {k: [c for c in cores if place(c) == k] for k in chips}
-    idle = {k: [c for c in range(WORLD) if place(c) == k and c not in cores] for k in chips}
+    free = {k: [c for c in range(WORLD) if place(c) == k and c not in cores] for k in chips}
     other = {c: [d for d in on[place(c)] if d != c][0] for c in cores}
     tile = {c: j for j, c in enumerate(cores)}
-    once = {k: [] for k in chips}
-    twice = {k: [] for k in chips}
-    reach, shut = {}, {}
+
+    def may(c, k):
+        return all(topo.may_write(c, d) for d in on[k])
+    own, helpers = {}, {}
+    for first in (True, False):
+        for s in cores:
+            k0 = place(s)
+            i = chips.index(k0)
+            ring = [chips[(i + 1 + t) % len(chips)] for t in range(len(chips) - 1)]
+            shut = [k for k in ring if not may(s, k)]
+            if bool(shut) != first:
+                continue
+            cand = sorted(free[k0], key=lambda h: (topo.die(h) == topo.die(s), h))
+            own[s], helpers[s] = [k for k in ring if k not in shut], []
+            if shut:
+                can = [h for h in cand if all(may(h, k) for k in shut)]
+                far = [h for h in can if topo.die(h) != topo.die(s)]
+                can = far if far else can
+                for h, part in zip(can, _split(shut, len(can))):
+                    helpers[s].append((h, part))
+                    free[k0].remove(h)
+            else:
+                for h in cand:
+                    ok = [k for k in own[s] if may(h, k)]
+                    if len(own[s]) > SELF and ok:
+                        helpers[s].append((h, [ok[-1]]))
+                        own[s].remove(ok[-1])
+                        free[k0].remove(h)
+    into = {k: [] for k in chips}
     for s in cores:
-        i = chips.index(place(s))
-        ring = [chips[(i + 1 + t) % len(chips)] for t in range(len(chips) - 1)]
-        reach[s] = [k for k in ring if all(topo.may_write(s, d) for d in on[k])]
-        shut[s] = [k for k in ring if k not in reach[s]]
-        for k in shut[s]:
-            twice[k].append(tile[s])
-    lent = {s: [] for s in cores}
-    for s in cores:
-        p = other[s]
-        for _ in range(MOVE):
-            can = [k for k in reach[s] if k in reach[p]]
-            if can and len(reach[s]) - len(reach[p]) - len(lent[p]) >= 2:
-                reach[s].remove(can[-1])
-                lent[p].append(can[-1])
-    for s in cores:
-        for turn, k in enumerate(reach[s]):
-            once[k].append((tile[s], turn))
-        for turn, k in enumerate(lent[s]):
-            once[k].append((tile[other[s]], len(reach[s]) + turn))
+        for t, k in enumerate(own[s]):
+            into[k].append((float(t), tile[s]))
+        for h, part in helpers[s]:
+            for t, k in enumerate(part):
+                into[k].append((HOP + t, tile[s]))
     land, ranks = {}, {}
     for k in chips:
-        lst = sorted(once[k])
-        half = (len(lst) + 1) // 2
-        for n, (j, turn) in enumerate(lst):
-            land[(k, j)] = on[k][0] if n < half else on[k][1]
-    for k in chips:
-        turn_of = dict(once[k])
         for c in on[k]:
-            mine = sorted([j for j, _ in once[k] if land[(k, j)] == c], key=lambda j: (turn_of[j], j))
-            ranks[c] = {"tile": tile[c], "partner": other[c], "mine": mine, "twice": sorted(twice[k]), "need": {}}
+            ranks[c] = {"tile": tile[c], "partner": other[c], "mine": [], "due": {}, "need": {}}
+        for n, (due, j) in enumerate(sorted(into[k])):
+            c = on[k][n % len(on[k])]
+            land[(k, j)] = c
+            ranks[c]["mine"].append(j)
+            ranks[c]["due"][j] = due
+            ranks[other[c]]["due"][j] = due + FWD
     for c in cores:
         e, p = ranks[c], ranks[other[c]]
-        order = [e["tile"]] + e["mine"] + [p["tile"]] + p["mine"] + e["twice"]
+        order = [e["tile"]] + e["mine"] + [p["tile"]] + p["mine"]
         e["slot"] = {j: n for n, j in enumerate(order)}
         e["theirs"] = list(p["mine"])
+        e["early"] = len([j for j in e["mine"] if e["due"][j] < HOP])
+        e["their_early"] = len([j for j in p["mine"] if p["due"][j] < HOP])
     relays = {}
     for s in cores:
-        e, j, pj, k = ranks[s], tile[s], tile[other[s]], place(s)
-        helpers = []
-        if shut[s]:
-            far = [d for kk in shut[s] for d in on[kk]]
-            can = [h for h in idle[k] if h not in relays and all(topo.may_write(h, d) for d in far)]
-            can.sort(key=lambda h: (topo.die(h) == topo.die(s), h))
-            for part in _split(far, min(len(can), (len(far) + PER_RELAY - 1) // PER_RELAY)):
-                h = can.pop(0)
-                bits = _common(topo, h, part)
-                bits = bits[:_pow2(len(bits))]
-                relays[h] = {"tile": j, "dsts": [(d, ranks[d]["slot"][j]) for d in part], "bits": bits}
-                for d in part:
-                    ranks[d]["need"][j] = len(bits)
-                helpers.append(h)
-        e["off"] = [(land[(kk, j)], ranks[land[(kk, j)]]["slot"][j]) for kk in reach[s]]
-        e["lent"] = [(land[(kk, pj)], ranks[land[(kk, pj)]]["slot"][pj]) for kk in lent[s]]
-        e["near"] = [(h, 0) for h in helpers] + [(other[s], ranks[other[s]]["slot"][j])]
-        off = _common(topo, s, [d for d, _ in e["off"] + e["lent"]])
-        off = off[:_pow2(len(off))]
-        near = [b for b in _common(topo, s, [d for d, _ in e["near"]]) if b not in off]
-        near = near[:_pow2(len(near))]
-        e["off_bits"], e["near_bits"] = off, near
+        e, j = ranks[s], tile[s]
+
+        def at(k):
+            return (land[(k, j)], ranks[land[(k, j)]]["slot"][j])
+        e["off"] = [at(k) for k in own[s]]
+        e["near"] = [(h, 0) for h, _ in helpers[s]] + [(other[s], ranks[other[s]]["slot"][j])]
+        e["off_bits"] = _common(topo, s, [d for d, _ in e["off"]])
+        near = [b for b in _common(topo, s, [d for d, _ in e["near"]]) if b not in e["off_bits"]]
+        e["near_bits"] = near[:_pow2(len(near))]
         for d, _ in e["off"]:
-            ranks[d]["need"][j] = len(off)
-        for d, _ in e["lent"]:
-            ranks[d]["need"][pj] = len(off)
-        ranks[other[s]]["need"][j] = len(near)
-        for h in helpers:
-            relays[h]["need"] = len(near)
-        fw = _common(topo, s, [other[s]])
-        e["fw_bits"] = fw[:_pow2(len(fw))]
+            ranks[d]["need"][j] = len(e["off_bits"])
+        ranks[other[s]]["need"][j] = len(e["near_bits"])
+        for h, part in helpers[s]:
+            dsts = [at(k) for k in part]
+            bits = _common(topo, h, [d for d, _ in dsts])
+            relays[h] = {"tile": j, "dsts": dsts, "bits": bits, "need": len(e["near_bits"])}
+            for d, _ in dsts:
+                ranks[d]["need"][j] = len(bits)
+        e["fw_bits"] = _common(topo, s, [other[s]])
         e["fw_slot"] = {t: ranks[other[s]]["slot"][t] for t in e["mine"]}
     return {"ranks": ranks, "relays": relays}
 
@@ -211,16 +212,6 @@ def _layer(g, T, x):
         V.quantize_mx(T.qc[:], T.qs[:], tl[:]).then_inc(S.vq, 1)
 
 
-def _runs(tiles):
-    out = []
-    for j in sorted(tiles):
-        if out and out[-1][-1] == j - 1:
-            out[-1].append(j)
-        else:
-            out.append([j])
-    return out
-
-
 def _rank(g, core, T, topo, e, pt):
     S, V, A, P, D = T.sem, g.vector, g.scalar, g.tensor, g.sync
     H = G * TILE // 2
@@ -228,8 +219,6 @@ def _rank(g, core, T, topo, e, pt):
     D.dma_start(T.xkb[:], T.xk[:]).then_inc(S.lxk, 16)
     A.dma_start(T.wkb[:, 0:H], T.wk[:, 0:H]).then_inc(S.lwk0, 16)
     D.dma_start(T.wkb[:, H:2 * H], T.wk[:, H:2 * H]).then_inc(S.lwk1, 16)
-    D.wait_ge(S.lxk, 16)
-    D.wait_ge(S.lwk1, 16)
     D.dma_start(T.xqb[:], T.xq[:]).then_inc(S.lxq, 16)
     D.dma_start(T.wqb[:, 0:H], T.wq[:, 0:H]).then_inc(S.lwq0, 16)
     D.dma_start(T.wqb[:, H:2 * H], T.wq[:, H:2 * H]).then_inc(S.lwq1, 16)
@@ -239,31 +228,34 @@ def _rank(g, core, T, topo, e, pt):
     for plane, sem in KINDS:
         _send(g, T, topo, core, plane, [(e["off_bits"], 0, e["off"], sem % me), (e["near_bits"], 0, e["near"], sem % me)], 1, sent)
     _layer(g, T, "q")
-    if e["lent"]:
-        for plane, sem in KINDS:
-            g.wait_ge(S[sem % pt], e["need"][pt])
-            _send(g, T, topo, core, plane, [(e["off_bits"], e["slot"][pt], e["lent"], sem % pt)], 1, sent)
-    for plane, sem in KINDS:
-        for b, part in enumerate(_split(e["mine"], BATCHES)):
-            for j in part:
-                g.wait_ge(S[sem % j], e["need"][j])
-            _send(g, T, topo, core, plane,
-                  [(e["fw_bits"], e["slot"][part[0]], [(e["partner"], e["fw_slot"][part[0]])], "fw%d" % b)], len(part), sent)
-    g.wait_ge(S.ls, sent[0])
-    came = {me: ("vk", 1)}
-    for j in [pt] + e["mine"] + e["twice"]:
-        came[j] = ("a%d" % j, e["need"][j])
-    for b, part in enumerate(_split(e["theirs"], BATCHES)):
+    mine, theirs = e["mine"], e["theirs"]
+
+    def onward(plane, part, sem):
         for j in part:
-            came[j] = ("fw%d" % b, 2 * len(e["fw_bits"]))
-    order = [me, pt] + e["mine"] + e["twice"] + e["theirs"]
+            g.wait_ge(S[KINDS[0 if plane else 1][1] % j], e["need"][j])
+        _send(g, T, topo, core, plane, [(e["fw_bits"], e["slot"][part[0]], [(e["partner"], e["fw_slot"][part[0]])], sem)],
+              len(part), sent)
+    for w, part in enumerate((mine[:e["early"]], mine[e["early"]:])):
+        if part:
+            onward(True, part, "fp%d" % w)
+        for j in part:
+            onward(False, [j], "fw%d" % mine.index(j))
+    g.wait_ge(S.ls, sent[0])
+    nfw = len(e["fw_bits"])
+    came = {me: [("vk", 1)]}
+    for j in [pt] + mine:
+        came[j] = [("s%d" % j, e["need"][j]), ("a%d" % j, e["need"][j])]
+    for t, j in enumerate(theirs):
+        came[j] = [("fp0" if t < e["their_early"] else "fp1", nfw), ("fw%d" % t, nfw)]
+    due = dict(e["due"])
+    due[me], due[pt] = -2.0, -1.0
+    order = sorted(due, key=lambda j: (due[j], j))
     P.wait_ge(S.vq, 1)
     P.wait_ge(S.ak, G)
     P.wait_ge(S.aq, G)
     for n, j in enumerate(order):
-        P.wait_ge(S[came[j][0]], came[j][1])
-        if came[j][0] == "a%d" % j:
-            P.wait_ge(S["s%d" % j], came[j][1])
+        for sem, val in came[j]:
+            P.wait_ge(S[sem], val)
         if n >= NBANK:
             P.wait_ge(S["cy%d" % order[n - NBANK]], 1)
         z = T.ps[:, BANK * (n % NBANK):BANK * (n % NBANK) + NC]
@@ -277,8 +269,13 @@ def _rank(g, core, T, topo, e, pt):
         else:
             A.wait_ge(S["my%d" % j], 1)
             A.activation(out, z, ActivationFunctionType.Copy).then_inc(S["cy%d" % j], 1)
-    runs = _runs([me, pt]) + _runs(e["mine"]) + _runs(e["twice"] + e["theirs"])
-    runs.sort(key=lambda r: max(order.index(j) for j in r))
+    runs = []
+    for n, j in enumerate(order):
+        r = runs[-1] if runs else None
+        if r and len(r) == 1 and n < len(order) - 2 and (j == r[0] + 1 or j == r[0] - 1):
+            runs[-1] = sorted(r + [j])
+        else:
+            runs.append([j])
     for r in runs:
         for j in r:
             D.wait_ge(S["cy%d" % j], 1)

from concourse.bass import DstId, RemoteDMATransfer
from concourse.mybir import dt, AluOpType, ActivationFunctionType

N, NC, G = 12, 128, 4
TILE = 4 * NC
WORLD = 256
CONST = 0.037
BANK, NBANK = 512, 8
SELF = 3
HOP, FWD = 3.0, 1.5

SCRATCH = {
    "xkb": ("sbuf", [128, TILE], "bfloat16"), "wkb": ("sbuf", [128, G * TILE], "bfloat16"),
    "xqb": ("sbuf", [128, TILE], "bfloat16"), "wqb": ("sbuf", [128, G * TILE], "bfloat16"),
    "xkc": ("sbuf", [128, NC], "float8_e4m3fn_x4"), "xks": ("sbuf", [128, NC], "uint8"),
    "wkc": ("sbuf", [128, G * NC], "float8_e4m3fn_x4"), "wks": ("sbuf", [128, G * NC], "uint8"),
    "xqc": ("sbuf", [128, NC], "float8_e4m3fn_x4"), "xqs": ("sbuf", [128, NC], "uint8"),
    "wqc": ("sbuf", [128, G * NC], "float8_e4m3fn_x4"), "wqs": ("sbuf", [128, G * NC], "uint8"),
    "kt": ("sbuf", [128, TILE], "bfloat16"), "qt": ("sbuf", [128, TILE], "bfloat16"),
    "kc": ("sbuf", [128, N * NC], "float8_e4m3fn_x4"), "ks": ("sbuf", [128, N * NC], "uint8"),
    "qc": ("sbuf", [128, NC], "float8_e4m3fn_x4"), "qs": ("sbuf", [128, NC], "uint8"),
    "ysb": ("sbuf", [128, N * NC], "float32"),
    "ps": ("psum", [128, NBANK * BANK], "float32"),
}
SEMAPHORES = (
    ["lxk", "lwk0", "lwk1", "lxq", "lwq0", "lwq1", "vxk", "vxq", "vk", "vq", "ak", "aq", "ls", "st", "fp0", "fp1"]
    + ["vwk%d" % i for i in range(G)] + ["vwq%d" % i for i in range(G)]
    + ["mk%d" % i for i in range(G)] + ["mq%d" % i for i in range(G)]
    + ["my%d" % j for j in range(N)] + ["cy%d" % j for j in range(N)]
    + ["a%d" % j for j in range(N)] + ["s%d" % j for j in range(N)] + ["fw%d" % b for b in range(N)]
)
KINDS = ((True, "s%d"), (False, "a%d"))
_MEMO = {}


def _bits(m):
    return [b for b in range(m.bit_length()) if (m >> b) & 1]


def _pow2(n):
    p = 1
    while p * 2 <= n:
        p *= 2
    return p


def _mask(bits):
    return sum(1 << b for b in bits)


def _common(topo, src, dsts):
    m = topo.mask(src, dsts[0])
    for d in dsts[1:]:
        m &= topo.mask(src, d)
    b = _bits(m)
    return b[:_pow2(len(b))]


def _split(seq, parts):
    parts = max(1, min(parts, len(seq)))
    out, at = [], 0
    for p in range(parts):
        n = (len(seq) - at + (parts - p) - 1) // (parts - p)
        out.append(seq[at:at + n])
        at += n
    return out


def _plan(topo, cores):
    def place(c):
        return (topo.host(c), topo.chip(c))
    chips = []
    for c in cores:
        if place(c) not in chips:
            chips.append(place(c))
    on = {k: [c for c in cores if place(c) == k] for k in chips}
    free = {k: [c for c in range(WORLD) if place(c) == k and c not in cores] for k in chips}
    other = {c: [d for d in on[place(c)] if d != c][0] for c in cores}
    tile = {c: j for j, c in enumerate(cores)}

    def may(c, k):
        return all(topo.may_write(c, d) for d in on[k])
    own, helpers = {}, {}
    for first in (True, False):
        for s in cores:
            k0 = place(s)
            i = chips.index(k0)
            ring = [chips[(i + 1 + t) % len(chips)] for t in range(len(chips) - 1)]
            shut = [k for k in ring if not may(s, k)]
            if bool(shut) != first:
                continue
            cand = sorted(free[k0], key=lambda h: (topo.die(h) == topo.die(s), h))
            own[s], helpers[s] = [k for k in ring if k not in shut], []
            if shut:
                can = [h for h in cand if all(may(h, k) for k in shut)]
                far = [h for h in can if topo.die(h) != topo.die(s)]
                can = far if far else can
                for h, part in zip(can, _split(shut, len(can))):
                    helpers[s].append((h, part))
                    free[k0].remove(h)
            else:
                for h in cand:
                    ok = [k for k in own[s] if may(h, k)]
                    if len(own[s]) > SELF and ok:
                        helpers[s].append((h, [ok[-1]]))
                        own[s].remove(ok[-1])
                        free[k0].remove(h)
    into = {k: [] for k in chips}
    for s in cores:
        for t, k in enumerate(own[s]):
            into[k].append((float(t), tile[s]))
        for h, part in helpers[s]:
            for t, k in enumerate(part):
                into[k].append((HOP + t, tile[s]))
    land, ranks = {}, {}
    for k in chips:
        for c in on[k]:
            ranks[c] = {"tile": tile[c], "partner": other[c], "mine": [], "due": {}, "need": {}}
        for n, (due, j) in enumerate(sorted(into[k])):
            c = on[k][n % len(on[k])]
            land[(k, j)] = c
            ranks[c]["mine"].append(j)
            ranks[c]["due"][j] = due
            ranks[other[c]]["due"][j] = due + FWD
    for c in cores:
        e, p = ranks[c], ranks[other[c]]
        order = [e["tile"]] + e["mine"] + [p["tile"]] + p["mine"]
        e["slot"] = {j: n for n, j in enumerate(order)}
        e["theirs"] = list(p["mine"])
        e["early"] = len([j for j in e["mine"] if e["due"][j] < HOP])
        e["their_early"] = len([j for j in p["mine"] if p["due"][j] < HOP])
    relays = {}
    for s in cores:
        e, j = ranks[s], tile[s]

        def at(k):
            return (land[(k, j)], ranks[land[(k, j)]]["slot"][j])
        e["off"] = [at(k) for k in own[s]]
        e["near"] = [(h, 0) for h, _ in helpers[s]] + [(other[s], ranks[other[s]]["slot"][j])]
        e["off_bits"] = _common(topo, s, [d for d, _ in e["off"]])
        near = [b for b in _common(topo, s, [d for d, _ in e["near"]]) if b not in e["off_bits"]]
        e["near_bits"] = near[:_pow2(len(near))]
        for d, _ in e["off"]:
            ranks[d]["need"][j] = len(e["off_bits"])
        ranks[other[s]]["need"][j] = len(e["near_bits"])
        for h, part in helpers[s]:
            dsts = [at(k) for k in part]
            bits = _common(topo, h, [d for d, _ in dsts])
            relays[h] = {"tile": j, "dsts": dsts, "bits": bits, "need": len(e["near_bits"])}
            for d, _ in dsts:
                ranks[d]["need"][j] = len(bits)
        e["fw_bits"] = _common(topo, s, [other[s]])
        e["fw_slot"] = {t: ranks[other[s]]["slot"][t] for t in e["mine"]}
    return {"ranks": ranks, "relays": relays}


def _view(T, plane, slot, width):
    a, b = NC * slot, NC * (slot + width)
    return T.ks[:, a:b] if plane else T.kc[:, a:b].bitcast(dt.uint8)


def _send(g, T, topo, core, plane, groups, width, sent):
    trs = []
    for bits, s0, dsts, sem in groups:
        ids = []
        for d, _ in dsts:
            rid, pid = topo.addr(d, core)
            ids.append(DstId(rid=rid, pnc=pid))
        trs.append(RemoteDMATransfer(dst_ids=ids, dma_engine_mask=_mask(bits), remote_sem=T.sem[sem],
                                     srcs=[_view(T, plane, s0, width)],
                                     dsts=[_view(T, plane, d0, width) for _, d0 in dsts]))
        sent[0] += len(bits)
    g.remote_dma_fused(trs, local_sem=T.sem.ls)


def _relay(g, core, T, topo, r):
    sent = [0]
    for plane, sem in KINDS:
        g.wait_ge(T.sem[sem % r["tile"]], r["need"])
        _send(g, T, topo, core, plane, [(r["bits"], 0, r["dsts"], sem % r["tile"])], 1, sent)
    g.wait_ge(T.sem.ls, sent[0])


def _layer(g, T, x):
    S, V, A, P = T.sem, g.vector, g.scalar, g.tensor
    xb, wb, xc, xs, wc, ws, tl = (T["x%sb" % x], T["w%sb" % x], T["x%sc" % x], T["x%ss" % x], T["w%sc" % x], T["w%ss" % x],
                                  T["%st" % x])
    base = 0 if x == "k" else G
    V.wait_ge(S["lx%s" % x], 16)
    V.quantize_mx(xc[:], xs[:], xb[:]).then_inc(S["vx%s" % x], 1)
    P.wait_ge(S["vx%s" % x], 1)
    for i in range(G):
        if i % 2 == 0:
            V.wait_ge(S["lw%s%d" % (x, i // 2)], 16)
        V.quantize_mx(wc[:, NC * i:NC * i + NC], ws[:, NC * i:NC * i + NC],
                      wb[:, TILE * i:TILE * i + TILE]).then_inc(S["vw%s%d" % (x, i)], 1)
        P.wait_ge(S["vw%s%d" % (x, i)], 1)
        P.matmul_mx(T.ps[:, BANK * (base + i):BANK * (base + i) + NC], wc[:, NC * i:NC * i + NC], ws[:, NC * i:NC * i + NC],
                    xc[:], xs[:], True, True).then_inc(S["m%s%d" % (x, i)], 1)
    for i in range(G):
        z = T.ps[:, BANK * (base + i):BANK * (base + i) + NC]
        if i % 2 == 0:
            A.wait_ge(S["m%s%d" % (x, i)], 1)
            A.activation(tl[:, i:TILE:4], z, ActivationFunctionType.Relu, scale=CONST).then_inc(S["a%s" % x], 1)
        else:
            V.wait_ge(S["m%s%d" % (x, i)], 1)
            V.tensor_scalar(tl[:, i:TILE:4], z, 0.0, CONST, AluOpType.max, AluOpType.mult).then_inc(S["a%s" % x], 1)
    V.wait_ge(S["a%s" % x], G)
    if x == "k":
        V.quantize_mx(T.kc[:, 0:NC], T.ks[:, 0:NC], tl[:]).then_inc(S.vk, 1)
    else:
        V.quantize_mx(T.qc[:], T.qs[:], tl[:]).then_inc(S.vq, 1)


def _rank(g, core, T, topo, e, pt):
    S, V, A, P, D = T.sem, g.vector, g.scalar, g.tensor, g.sync
    H = G * TILE // 2
    me = e["tile"]
    D.dma_start(T.xkb[:], T.xk[:]).then_inc(S.lxk, 16)
    A.dma_start(T.wkb[:, 0:H], T.wk[:, 0:H]).then_inc(S.lwk0, 16)
    D.dma_start(T.wkb[:, H:2 * H], T.wk[:, H:2 * H]).then_inc(S.lwk1, 16)
    D.dma_start(T.xqb[:], T.xq[:]).then_inc(S.lxq, 16)
    D.dma_start(T.wqb[:, 0:H], T.wq[:, 0:H]).then_inc(S.lwq0, 16)
    D.dma_start(T.wqb[:, H:2 * H], T.wq[:, H:2 * H]).then_inc(S.lwq1, 16)
    _layer(g, T, "k")
    sent = [0]
    g.wait_ge(S.vk, 1)
    for plane, sem in KINDS:
        _send(g, T, topo, core, plane, [(e["off_bits"], 0, e["off"], sem % me), (e["near_bits"], 0, e["near"], sem % me)], 1, sent)
    _layer(g, T, "q")
    mine, theirs = e["mine"], e["theirs"]

    def onward(plane, part, sem):
        for j in part:
            g.wait_ge(S[KINDS[0 if plane else 1][1] % j], e["need"][j])
        _send(g, T, topo, core, plane, [(e["fw_bits"], e["slot"][part[0]], [(e["partner"], e["fw_slot"][part[0]])], sem)],
              len(part), sent)
    for w, part in enumerate((mine[:e["early"]], mine[e["early"]:])):
        if part:
            onward(True, part, "fp%d" % w)
        for j in part:
            onward(False, [j], "fw%d" % mine.index(j))
    g.wait_ge(S.ls, sent[0])
    nfw = len(e["fw_bits"])
    came = {me: [("vk", 1)]}
    for j in [pt] + mine:
        came[j] = [("s%d" % j, e["need"][j]), ("a%d" % j, e["need"][j])]
    for t, j in enumerate(theirs):
        came[j] = [("fp0" if t < e["their_early"] else "fp1", nfw), ("fw%d" % t, nfw)]
    due = dict(e["due"])
    due[me], due[pt] = -2.0, -1.0
    order = sorted(due, key=lambda j: (due[j], j))
    P.wait_ge(S.vq, 1)
    P.wait_ge(S.ak, G)
    P.wait_ge(S.aq, G)
    for n, j in enumerate(order):
        for sem, val in came[j]:
            P.wait_ge(S[sem], val)
        if n >= NBANK:
            P.wait_ge(S["cy%d" % order[n - NBANK]], 1)
        z = T.ps[:, BANK * (n % NBANK):BANK * (n % NBANK) + NC]
        s = e["slot"][j]
        P.matmul_mx(z, T.kc[:, NC * s:NC * s + NC], T.ks[:, NC * s:NC * s + NC], T.qc[:], T.qs[:], True, True
                    ).then_inc(S["my%d" % j], 1)
        out = T.ysb[:, NC * j:NC * j + NC]
        if n % 2 == 0:
            V.wait_ge(S["my%d" % j], 1)
            V.tensor_copy(out, z).then_inc(S["cy%d" % j], 1)
        else:
            A.wait_ge(S["my%d" % j], 1)
            A.activation(out, z, ActivationFunctionType.Copy).then_inc(S["cy%d" % j], 1)
    runs = []
    for n, j in enumerate(order):
        r = runs[-1] if runs else None
        if r and len(r) == 1 and n < len(order) - 2 and (j == r[0] + 1 or j == r[0] - 1):
            runs[-1] = sorted(r + [j])
        else:
            runs.append([j])
    for r in runs:
        for j in r:
            D.wait_ge(S["cy%d" % j], 1)
        D.dma_start(T.y[:, NC * r[0]:NC * r[-1] + NC], T.ysb[:, NC * r[0]:NC * r[-1] + NC]).then_inc(S.st, 16)
    D.wait_ge(S.st, 16 * len(runs))


def rank_program(g, core, T, topo):
    if "plan" not in _MEMO:
        _MEMO["plan"] = _plan(topo, list(T.cores))
    plan = _MEMO["plan"]
    if core in plan["relays"]:
        _relay(g, core, T, topo, plan["relays"][core])
    elif core in plan["ranks"]:
        e = plan["ranks"][core]
        _rank(g, core, T, topo, e, plan["ranks"][e["partner"]]["tile"])
